import numpy as np
import ml_dtypes


def mxq(x, axis, fmt="e4m3"):
    dtype, down = {"e4m3": (ml_dtypes.float8_e4m3fn, 7), "e5m2": (ml_dtypes.float8_e5m2, 14)}[fmt]
    v = np.moveaxis(np.asarray(x, np.float32).astype(ml_dtypes.bfloat16).astype(np.float64), axis, -1)
    blocks = v.reshape(v.shape[:-1] + (-1, 32))
    amax = np.abs(blocks).max(-1, keepdims=True)
    byte = np.maximum(np.where(amax > 0, np.frexp(amax)[1] - 1 + 127, 0) - down, 1)
    scale = np.exp2(byte - 127.0)
    codes = (blocks / scale).astype(np.float32).astype(dtype).astype(np.float64)
    return np.moveaxis((codes * scale).reshape(v.shape), -1, axis)


WIDE = False


def mx_kscale(k, group=512):
    if not WIDE:
        return np.ones(k)
    levels = np.array([18, -18])
    if group != 512:
        return np.exp2(np.random.permutation(np.resize(levels, k // group))).repeat(group)
    if k % 512:
        return np.exp2(np.random.permutation(np.resize(levels, k // 32))).repeat(32)
    a = np.empty((k // 512, 16))
    for p in range(k // 512):
        a[p, :8] = np.random.permutation(np.resize(levels, 8))
        for g in range(8):
            far = levels[np.abs(levels - a[p, g]) >= 10]
            a[p, g + 8] = far[np.random.randint(len(far))]
    return np.exp2(a.ravel()).repeat(32)


def f64(x):
    return np.asarray(x).astype(np.float64)


G, D, M, O, N = 4, 128, 128, 128, 512


def sgn(shape):
    return np.random.uniform(0.5, 2.0, shape) * np.where(np.random.standard_normal(shape) < 0, -1.0, 1.0)


def setup_inputs():
    n = np.random.standard_normal
    s_d = mx_kscale(D, 0)
    s_m = mx_kscale(M, 0)
    return {
        "x": (n((G, D, N)) * s_d[:, None]).astype(np.float32),
        "w1": (n((G, D, M)) / np.sqrt(D) / s_d[:, None]).astype(np.float32),
        "w2": (n((G, D, M)) / np.sqrt(D) / s_d[:, None]).astype(np.float32),
        "gn": (np.random.uniform(0.5, 2.0, (G, M, 1))).astype(np.float32),
        "hs": (sgn((G, M, 1)) * s_m[:, None]).astype(np.float32),
        "wo2": (n((G, M, O)) / np.sqrt(M) / s_m[:, None]).astype(np.float32),
        "res": (0.5 * n((G, O, N))).astype(np.float32),
    }


def reference(x, w1, w2, gn, hs, wo2, res):
    w1q = mxq(f64(w1), 1, "e4m3")
    xq = mxq(f64(x), 1, "e4m3")
    z1 = w1q.transpose(0, 2, 1) @ xq
    w2q = mxq(f64(w2), 1, "e4m3")
    z2 = w2q.transpose(0, 2, 1) @ xq
    mu = np.mean(z1, axis=-1, keepdims=True)
    ce = z1 - mu
    sd = np.sqrt(np.mean(np.square(ce), axis=-1, keepdims=True) + 0.05)
    h = np.tanh(ce / sd * f64(gn)) * z2
    hh = h * f64(hs)
    wo2q = mxq(f64(wo2), 1, "e4m3")
    hhq = mxq(hh, 1, "e4m3")
    y0 = wo2q.transpose(0, 2, 1) @ hhq
    y = y0 + f64(res)
    return y

@@ -1,0 +1,225 @@
+from contextlib import ExitStack
+
+import concourse.mybir as mybir
+
+G, D, M, O, N = 4, 128, 128, 128, 512
+FLOPS = 2 * G * N * (2 * D * M + M * O)
+
+F32 = mybir.dt.float32
+BF16 = mybir.dt.bfloat16
+U32 = mybir.dt.uint32
+U8 = mybir.dt.uint8
+FP8X4 = mybir.dt.float8_e4m3fn_x4
+ACT = mybir.ActivationFunctionType
+ALU = mybir.AluOpType
+
+P = 128
+ROWS = 32
+PACK = 4
+HALVES = 2
+HALF = N // HALVES
+MM_N = 128
+EPS = 0.05
+X_SPLIT = 128
+H_SPLIT = 160
+
+
+def tile_rows_frowcentre_kernel(tc, x, w1, w2, gn, hs, wo2, res, out):
+    nc = tc.nc
+    with ExitStack() as ctx:
+        sb = ctx.enter_context(tc.tile_pool(name="sb", bufs=1))
+        ps = ctx.enter_context(tc.psum_pool(name="ps", bufs=1))
+        ctx.enter_context(tc.manual_schedule())
+
+        def sbt(name, shape, dtype):
+            return sb.tile(shape, dtype, name=name, align_bytes=64)
+
+        def interleave(copy, dst, src, c0, c1):
+            copy(
+                out=dst[:, c0:c1, :].rearrange("p (c i) t -> p c t i", i=4),
+                in_=src[:, :, c0:c1].rearrange("p t (c i) -> p c t i", i=4),
+            )
+
+        def quantize(name, words, width):
+            codes = sbt(name + "_codes", [P, width], U32)
+            scales = sbt(name + "_scales", [P, width], U8)
+            nc.vector.quantize_mx(
+                out=codes[:].bitcast(FP8X4),
+                scales=scales[:],
+                in_=words[:].rearrange("p c t -> p (c t)"),
+            )
+            return codes, scales
+
+        def product(dst, col0, g, weights, moving):
+            rows = slice(ROWS * g, ROWS * (g + 1))
+            for c in range(0, HALF, MM_N):
+                nc.tensor.matmul_mx(
+                    out=dst[:, col0 + c : col0 + c + MM_N],
+                    lhsT=weights[0][rows, :].bitcast(FP8X4),
+                    lhsT_scale=weights[1][rows, :],
+                    rhs=moving[0][rows, c : c + MM_N].bitcast(FP8X4),
+                    rhs_scale=moving[1][rows, c : c + MM_N],
+                    start=True,
+                    stop=True,
+                )
+
+        def load_packed(name, src, c0, c1):
+            raw = sbt(name, [P, PACK, c1 - c0], F32)
+            nc.sync.dma_start(out=raw[:], in_=src.rearrange("g (p t) c -> (g p) t c", t=PACK)[:, :, c0:c1])
+            return raw
+
+        vec_rows = sbt("vec_rows", [P, G * ROWS], F32)
+        nc.gpsimd.memset(vec_rows[:], 0.0)
+        minus_half = sbt("minus_half", [P, 1], F32)
+        nc.gpsimd.memset(minus_half[:], -0.5)
+        w1_raw = load_packed("w1_raw", w1, 0, M)
+        x_raw = [load_packed("x_raw%d" % h, x, h * HALF, (h + 1) * HALF) for h in range(HALVES)]
+        for row, vec in ((0, gn), (2, hs)):
+            nc.sync.dma_start(
+                out=vec_rows[row:P:ROWS, :].rearrange("q (g c) -> q g c", c=ROWS),
+                in_=vec.rearrange("g (q c) o -> q g (c o)", c=ROWS),
+            )
+        w2_raw = load_packed("w2_raw", w2, 0, M)
+        wo_raw = load_packed("wo_raw", wo2, 0, O)
+        res_sb = sbt("res_sb", [P, G, N], F32)
+        nc.sync.dma_start(out=res_sb[:], in_=res.rearrange("g o n -> o g n"))
+
+        bank = [[ps.tile([P, 2 * HALF], F32, name="bank%d%d" % (g, h)) for h in range(HALVES)] for g in range(G)]
+
+        w1_words = sbt("w1_words", [P, M, PACK], BF16)
+        interleave(nc.vector.tensor_copy, w1_words, w1_raw, 0, M)
+        vecs = sbt("vecs", [P, G * ROWS], F32)
+        w1q = quantize("w1", w1_words, M)
+
+        x_words = [sbt("x_words%d" % h, [P, HALF, PACK], BF16) for h in range(HALVES)]
+        xq = [None] * HALVES
+        stats = [sbt("stats%d" % g, [P, HALVES, 6], F32) for g in range(G)]
+        mean_var = [sbt("mean_var%d" % g, [P, 2], F32) for g in range(G)]
+        var_eps = [sbt("var_eps%d" % g, [P, 1], F32) for g in range(G)]
+        rstd = [sbt("rstd%d" % g, [P, 1], F32) for g in range(G)]
+        affine = [sbt("affine%d" % g, [P, 2], F32) for g in range(G)]
+        gate = [[sbt("gate%d%d" % (g, h), [P, HALF], F32) for h in range(HALVES)] for g in range(G)]
+        hh = [[sbt("hh%d%d" % (g, h), [P, HALF], BF16) for h in range(HALVES)] for g in range(G)]
+        hh_rows = [sbt("hh_rows%d" % h, [P, PACK, HALF], BF16) for h in range(HALVES)]
+        hh_words = [sbt("hh_words%d" % h, [P, HALF, PACK], BF16) for h in range(HALVES)]
+        hq = [None] * HALVES
+
+        def x_interleave(h):
+            interleave(nc.scalar.copy, x_words[h], x_raw[h], X_SPLIT, HALF)
+            interleave(nc.vector.tensor_copy, x_words[h], x_raw[h], 0, X_SPLIT)
+
+        def x_first(h):
+            xq[h] = quantize("x%d" % h, x_words[h], HALF)
+            for g in range(G):
+                product(bank[g][h], 0, g, w1q, xq[h])
+
+        def row_stats(g, h):
+            nc.vector.bn_stats(out=stats[g][:, h, :], in_=bank[g][h][:, 0:HALF])
+
+        def second(g, h):
+            product(bank[g][h], HALF, g, w2q, xq[h])
+
+        def aggregate(g):
+            nc.vector.bn_aggr(out=mean_var[g][:], in_=stats[g][:].rearrange("p h s -> p (h s)"))
+
+        def spread(g):
+            nc.scalar.activation(out=var_eps[g][:], in_=mean_var[g][:, 1:2], func=ACT.Copy, bias=EPS)
+            nc.gpsimd.tensor_scalar(
+                out=vecs[:, ROWS * g + 1 : ROWS * g + 2], in0=mean_var[g][:, 0:1],
+                scalar1=vecs[:, ROWS * g : ROWS * g + 1], scalar2=-1.0, op0=ALU.mult, op1=ALU.mult,
+            )
+            nc.gpsimd.tensor_tensor(out=rstd[g][:], in0=var_eps[g][:], in1=minus_half[:], op=ALU.pow)
+
+        def fold(g):
+            nc.scalar.activation(out=affine[g][:], in_=vecs[:, ROWS * g : ROWS * g + 2], func=ACT.Copy, scale=rstd[g][:])
+
+        def tanh(g, h):
+            nc.scalar.activation(
+                out=gate[g][h][:], in_=bank[g][h][:, 0:HALF], func=ACT.Tanh,
+                scale=affine[g][:, 0:1], bias=affine[g][:, 1:2],
+            )
+
+        def hidden(g, h):
+            nc.vector.scalar_tensor_tensor(
+                out=hh[g][h][:], in0=gate[g][h][:], scalar=vecs[:, ROWS * g + 2 : ROWS * g + 3],
+                in1=bank[g][h][:, HALF : 2 * HALF], op0=ALU.mult, op1=ALU.mult,
+            )
+            nc.sync.dma_start(out=hh_rows[h][ROWS * g : ROWS * (g + 1), :, :], in_=hh[g][h][:])
+
+        def h_interleave(h):
+            interleave(nc.scalar.copy, hh_words[h], hh_rows[h], H_SPLIT, HALF)
+            interleave(nc.vector.tensor_copy, hh_words[h], hh_rows[h], 0, H_SPLIT)
+
+        def h_product(h):
+            hq[h] = quantize("h%d" % h, hh_words[h], HALF)
+            for g in range(G):
+                product(bank[g][h], 0, g, woq, hq[h])
+
+        def finish(g, h):
+            cols = slice(h * HALF, (h + 1) * HALF)
+            y = sbt("y%d%d" % (g, h), [P, HALF], F32)
+            nc.vector.tensor_tensor(out=y[:], in0=bank[g][h][:, 0:HALF], in1=res_sb[:, g, cols], op=ALU.add)
+            nc.sync.dma_start(out=out[g, :, cols], in_=y[:])
+
+        x_interleave(0)
+        x_first(0)
+        x_interleave(1)
+        nc.vector.transpose(vecs[:], vec_rows[:])
+        row_stats(0, 0)
+        x_first(1)
+        w2_words = sbt("w2_words", [P, M, PACK], BF16)
+        interleave(nc.scalar.copy, w2_words, w2_raw, 0, M)
+        wo_words = sbt("wo_words", [P, O, PACK], BF16)
+        interleave(nc.scalar.copy, wo_words, wo_raw, 0, O)
+        row_stats(1, 0)
+        w2q = quantize("w2", w2_words, M)
+        row_stats(0, 1)
+        row_stats(1, 1)
+        for h in range(HALVES):
+            second(0, h)
+            second(1, h)
+        aggregate(0)
+        spread(0)
+        row_stats(2, 0)
+        second(2, 0)
+        aggregate(1)
+        spread(1)
+        row_stats(2, 1)
+        second(2, 1)
+        fold(0)
+        tanh(0, 0)
+        row_stats(3, 0)
+        second(3, 0)
+        aggregate(2)
+        spread(2)
+        row_stats(3, 1)
+        second(3, 1)
+        fold(1)
+        tanh(1, 0)
+        hidden(0, 0)
+        aggregate(3)
+        spread(3)
+        hidden(1, 0)
+        fold(2)
+        tanh(0, 1)
+        tanh(2, 0)
+        hidden(2, 0)
+        fold(3)
+        tanh(1, 1)
+        tanh(3, 0)
+        hidden(0, 1)
+        hidden(3, 0)
+        hidden(1, 1)
+        for g in range(2, G):
+            tanh(g, 1)
+            hidden(g, 1)
+        woq = quantize("wo", wo_words, O)
+        h_interleave(0)
+        h_product(0)
+        h_interleave(1)
+        finish(0, 0)
+        h_product(1)
+        for g in range(1, G):
+            finish(g, 0)
+        for g in range(G):
+            finish(g, 1)

@@ -20,8 +20,8 @@ HALVES = 2
 HALF = N // HALVES
 MM_N = 128
 EPS = 0.05
-X_SPLIT = 128
-H_SPLIT = 160
+X_VECTOR = 176
+H_VECTOR = (160, 104)
 
 
 def tile_rows_frowcentre_kernel(tc, x, w1, w2, gn, hs, wo2, res, out):
@@ -70,90 +70,97 @@ def tile_rows_frowcentre_kernel(tc, x, w1, w2, gn, hs, wo2, res, out):
 
         vec_rows = sbt("vec_rows", [P, G * ROWS], F32)
         nc.gpsimd.memset(vec_rows[:], 0.0)
-        minus_half = sbt("minus_half", [P, 1], F32)
+        minus_half = sbt("minus_half", [P, 2], F32)
         nc.gpsimd.memset(minus_half[:], -0.5)
         w1_raw = load_packed("w1_raw", w1, 0, M)
-        x_raw = [load_packed("x_raw%d" % h, x, h * HALF, (h + 1) * HALF) for h in range(HALVES)]
+        x_raw = [load_packed("x_raw0", x, 0, HALF)]
         for row, vec in ((0, gn), (2, hs)):
             nc.sync.dma_start(
                 out=vec_rows[row:P:ROWS, :].rearrange("q (g c) -> q g c", c=ROWS),
                 in_=vec.rearrange("g (q c) o -> q g (c o)", c=ROWS),
             )
+        x_raw.append(load_packed("x_raw1", x, HALF, N))
         w2_raw = load_packed("w2_raw", w2, 0, M)
         wo_raw = load_packed("wo_raw", wo2, 0, O)
         res_sb = sbt("res_sb", [P, G, N], F32)
         nc.sync.dma_start(out=res_sb[:], in_=res.rearrange("g o n -> o g n"))
 
-        bank = [[ps.tile([P, 2 * HALF], F32, name="bank%d%d" % (g, h)) for h in range(HALVES)] for g in range(G)]
+        bank = [[ps.tile([P, N], F32, name="bank%d%d" % (g, i)) for i in range(2)] for g in range(G)]
 
+        vecs = sbt("vecs", [P, G * ROWS], F32)
         w1_words = sbt("w1_words", [P, M, PACK], BF16)
         interleave(nc.vector.tensor_copy, w1_words, w1_raw, 0, M)
-        vecs = sbt("vecs", [P, G * ROWS], F32)
+        minus_gn = sbt("minus_gn", [P, G - 1], F32)
         w1q = quantize("w1", w1_words, M)
 
         x_words = [sbt("x_words%d" % h, [P, HALF, PACK], BF16) for h in range(HALVES)]
         xq = [None] * HALVES
-        stats = [sbt("stats%d" % g, [P, HALVES, 6], F32) for g in range(G)]
-        mean_var = [sbt("mean_var%d" % g, [P, 2], F32) for g in range(G)]
-        var_eps = [sbt("var_eps%d" % g, [P, 1], F32) for g in range(G)]
-        rstd = [sbt("rstd%d" % g, [P, 1], F32) for g in range(G)]
+        stats = [sbt("stats%d" % g, [P, 16], F32) for g in range(G)]
+        mean_var = sbt("mean_var", [P, G, 2], F32)
+        rstd = sbt("rstd", [P, G], F32)
         affine = [sbt("affine%d" % g, [P, 2], F32) for g in range(G)]
-        gate = [[sbt("gate%d%d" % (g, h), [P, HALF], F32) for h in range(HALVES)] for g in range(G)]
-        hh = [[sbt("hh%d%d" % (g, h), [P, HALF], BF16) for h in range(HALVES)] for g in range(G)]
-        hh_rows = [sbt("hh_rows%d" % h, [P, PACK, HALF], BF16) for h in range(HALVES)]
+        gate = [sbt("gate%d" % g, [P, N], F32) for g in range(G)]
+        hh = [sbt("hh%d" % g, [P, N], BF16) for g in range(G)]
+        hh_rows = sbt("hh_rows", [P, PACK, N], BF16)
         hh_words = [sbt("hh_words%d" % h, [P, HALF, PACK], BF16) for h in range(HALVES)]
-        hq = [None] * HALVES
 
         def x_interleave(h):
-            interleave(nc.scalar.copy, x_words[h], x_raw[h], X_SPLIT, HALF)
-            interleave(nc.vector.tensor_copy, x_words[h], x_raw[h], 0, X_SPLIT)
+            interleave(nc.scalar.copy, x_words[h], x_raw[h], X_VECTOR, HALF)
+            interleave(nc.vector.tensor_copy, x_words[h], x_raw[h], 0, X_VECTOR)
 
-        def x_first(h):
-            xq[h] = quantize("x%d" % h, x_words[h], HALF)
-            for g in range(G):
-                product(bank[g][h], 0, g, w1q, xq[h])
-
-        def row_stats(g, h):
-            nc.vector.bn_stats(out=stats[g][:, h, :], in_=bank[g][h][:, 0:HALF])
+        def first(g, h):
+            product(bank[g][0], h * HALF, g, w1q, xq[h])
 
         def second(g, h):
-            product(bank[g][h], HALF, g, w2q, xq[h])
+            product(bank[g][1], h * HALF, g, w2q, xq[h])
+
+        def row_stats(g, h):
+            nc.vector.bn_stats(out=stats[g][:, 2 + 6 * h : 8 + 6 * h], in_=bank[g][0][:, h * HALF : (h + 1) * HALF])
+
+        def add_eps(g):
+            nc.scalar.activation(out=stats[g][:, 4:5], in_=stats[g][:, 4:5], func=ACT.Copy, bias=EPS * N)
 
         def aggregate(g):
-            nc.vector.bn_aggr(out=mean_var[g][:], in_=stats[g][:].rearrange("p h s -> p (h s)"))
+            nc.vector.bn_aggr(out=mean_var[:, g, :], in_=stats[g][:, 2:14])
 
-        def spread(g):
-            nc.scalar.activation(out=var_eps[g][:], in_=mean_var[g][:, 1:2], func=ACT.Copy, bias=EPS)
-            nc.gpsimd.tensor_scalar(
-                out=vecs[:, ROWS * g + 1 : ROWS * g + 2], in0=mean_var[g][:, 0:1],
-                scalar1=vecs[:, ROWS * g : ROWS * g + 1], scalar2=-1.0, op0=ALU.mult, op1=ALU.mult,
+        def shift(g):
+            nc.scalar.activation(
+                out=vecs[:, ROWS * g + 1 : ROWS * g + 2], in_=mean_var[:, g, 0:1], func=ACT.Copy,
+                scale=minus_gn[:, g : g + 1],
             )
-            nc.gpsimd.tensor_tensor(out=rstd[g][:], in0=var_eps[g][:], in1=minus_half[:], op=ALU.pow)
+
+        def spread(g0, g1):
+            nc.gpsimd.tensor_tensor(
+                out=rstd[:, g0:g1], in0=mean_var[:, g0:g1, 1], in1=minus_half[:, 0 : g1 - g0], op=ALU.pow
+            )
 
         def fold(g):
-            nc.scalar.activation(out=affine[g][:], in_=vecs[:, ROWS * g : ROWS * g + 2], func=ACT.Copy, scale=rstd[g][:])
-
-        def tanh(g, h):
             nc.scalar.activation(
-                out=gate[g][h][:], in_=bank[g][h][:, 0:HALF], func=ACT.Tanh,
-                scale=affine[g][:, 0:1], bias=affine[g][:, 1:2],
+                out=affine[g][:], in_=vecs[:, ROWS * g : ROWS * g + 2], func=ACT.Copy, scale=rstd[:, g : g + 1]
             )
 
-        def hidden(g, h):
-            nc.vector.scalar_tensor_tensor(
-                out=hh[g][h][:], in0=gate[g][h][:], scalar=vecs[:, ROWS * g + 2 : ROWS * g + 3],
-                in1=bank[g][h][:, HALF : 2 * HALF], op0=ALU.mult, op1=ALU.mult,
+        def tanh(g, c0, c1):
+            nc.scalar.activation(
+                out=gate[g][:, c0:c1], in_=bank[g][0][:, c0:c1],
+                func=ACT.Tanh, scale=affine[g][:, 0:1], bias=affine[g][:, 1:2],
             )
-            nc.sync.dma_start(out=hh_rows[h][ROWS * g : ROWS * (g + 1), :, :], in_=hh[g][h][:])
+
+        def hidden(g, c0, c1):
+            nc.vector.scalar_tensor_tensor(
+                out=hh[g][:, c0:c1], in0=gate[g][:, c0:c1], scalar=vecs[:, ROWS * g + 2 : ROWS * g + 3],
+                in1=bank[g][1][:, c0:c1], op0=ALU.mult, op1=ALU.mult,
+            )
+            nc.sync.dma_start(out=hh_rows[ROWS * g : ROWS * (g + 1), :, c0:c1], in_=hh[g][:, c0:c1])
 
         def h_interleave(h):
-            interleave(nc.scalar.copy, hh_words[h], hh_rows[h], H_SPLIT, HALF)
-            interleave(nc.vector.tensor_copy, hh_words[h], hh_rows[h], 0, H_SPLIT)
+            rows = hh_rows[:, :, h * HALF : (h + 1) * HALF]
+            interleave(nc.scalar.copy, hh_words[h], rows, H_VECTOR[h], HALF)
+            interleave(nc.vector.tensor_copy, hh_words[h], rows, 0, H_VECTOR[h])
 
-        def h_product(h):
-            hq[h] = quantize("h%d" % h, hh_words[h], HALF)
+        def third(h):
+            hq = quantize("h%d" % h, hh_words[h], HALF)
             for g in range(G):
-                product(bank[g][h], 0, g, woq, hq[h])
+                product(bank[g][h], 0, g, woq, hq)
 
         def finish(g, h):
             cols = slice(h * HALF, (h + 1) * HALF)
@@ -162,63 +169,73 @@ def tile_rows_frowcentre_kernel(tc, x, w1, w2, gn, hs, wo2, res, out):
             nc.sync.dma_start(out=out[g, :, cols], in_=y[:])
 
         x_interleave(0)
-        x_first(0)
-        x_interleave(1)
+        xq[0] = quantize("x0", x_words[0], HALF)
+        for g in range(G):
+            first(g, 0)
         nc.vector.transpose(vecs[:], vec_rows[:])
+        nc.gpsimd.tensor_scalar(
+            out=minus_gn[:], in0=vecs[:, 0 : (G - 1) * ROWS : ROWS], scalar1=-1.0, scalar2=0.0, op0=ALU.mult, op1=ALU.add
+        )
+        x_interleave(1)
         row_stats(0, 0)
-        x_first(1)
+        xq[1] = quantize("x1", x_words[1], HALF)
+        row_stats(1, 0)
+        row_stats(2, 0)
+        for g in (0, 1, 3, 2):
+            first(g, 1)
         w2_words = sbt("w2_words", [P, M, PACK], BF16)
         interleave(nc.scalar.copy, w2_words, w2_raw, 0, M)
+        add_eps(0)
+        add_eps(1)
         wo_words = sbt("wo_words", [P, O, PACK], BF16)
         interleave(nc.scalar.copy, wo_words, wo_raw, 0, O)
-        row_stats(1, 0)
-        w2q = quantize("w2", w2_words, M)
+        add_eps(2)
         row_stats(0, 1)
         row_stats(1, 1)
-        for h in range(HALVES):
-            second(0, h)
-            second(1, h)
         aggregate(0)
-        spread(0)
-        row_stats(2, 0)
-        second(2, 0)
-        aggregate(1)
-        spread(1)
+        shift(0)
+        spread(0, 1)
         row_stats(2, 1)
-        second(2, 1)
-        fold(0)
-        tanh(0, 0)
+        aggregate(1)
+        shift(1)
         row_stats(3, 0)
-        second(3, 0)
+        add_eps(3)
         aggregate(2)
-        spread(2)
+        shift(2)
+        spread(1, 3)
         row_stats(3, 1)
-        second(3, 1)
-        fold(1)
-        tanh(1, 0)
-        hidden(0, 0)
+        fold(0)
+        w2q = quantize("w2", w2_words, M)
         aggregate(3)
-        spread(3)
-        hidden(1, 0)
+        spread(3, 4)
+        last = ROWS * (G - 1)
+        nc.gpsimd.tensor_scalar(
+            out=vecs[:, last + 1 : last + 2], in0=mean_var[:, G - 1, 0:1],
+            scalar1=vecs[:, last : last + 1], scalar2=-1.0, op0=ALU.mult, op1=ALU.mult,
+        )
+        nc.gpsimd.tensor_scalar(
+            out=affine[G - 1][:], in0=vecs[:, last : last + 2],
+            scalar1=rstd[:, G - 1 : G], scalar2=1.0, op0=ALU.mult, op1=ALU.mult,
+        )
+        second(0, 0)
+        second(0, 1)
+        for h in range(HALVES):
+            for g in range(1, G):
+                second(g, h)
+        tanh(0, 0, N)
+        fold(1)
         fold(2)
-        tanh(0, 1)
-        tanh(2, 0)
-        hidden(2, 0)
-        fold(3)
-        tanh(1, 1)
-        tanh(3, 0)
-        hidden(0, 1)
-        hidden(3, 0)
-        hidden(1, 1)
-        for g in range(2, G):
-            tanh(g, 1)
-            hidden(g, 1)
+        hidden(0, 0, N)
+        for h in range(HALVES):
+            for g in range(1, G):
+                tanh(g, h * HALF, (h + 1) * HALF)
+                hidden(g, h * HALF, (h + 1) * HALF)
         woq = quantize("wo", wo_words, O)
         h_interleave(0)
-        h_product(0)
+        third(0)
         h_interleave(1)
         finish(0, 0)
-        h_product(1)
+        third(1)
         for g in range(1, G):
             finish(g, 0)
         for g in range(G):

@@ -21,7 +21,7 @@ HALF = N // HALVES
 MM_N = 128
 EPS = 0.05
 X_VECTOR = 176
-H_VECTOR = (160, 104)
+H_VECTOR = (160, 160)
 
 
 def tile_rows_frowcentre_kernel(tc, x, w1, w2, gn, hs, wo2, res, out):
@@ -90,7 +90,7 @@ def tile_rows_frowcentre_kernel(tc, x, w1, w2, gn, hs, wo2, res, out):
         vecs = sbt("vecs", [P, G * ROWS], F32)
         w1_words = sbt("w1_words", [P, M, PACK], BF16)
         interleave(nc.vector.tensor_copy, w1_words, w1_raw, 0, M)
-        minus_gn = sbt("minus_gn", [P, G - 1], F32)
+        minus_gn = sbt("minus_gn", [P, G], F32)
         w1q = quantize("w1", w1_words, M)
 
         x_words = [sbt("x_words%d" % h, [P, HALF, PACK], BF16) for h in range(HALVES)]
@@ -173,23 +173,29 @@ def tile_rows_frowcentre_kernel(tc, x, w1, w2, gn, hs, wo2, res, out):
         for g in range(G):
             first(g, 0)
         nc.vector.transpose(vecs[:], vec_rows[:])
-        nc.gpsimd.tensor_scalar(
-            out=minus_gn[:], in0=vecs[:, 0 : (G - 1) * ROWS : ROWS], scalar1=-1.0, scalar2=0.0, op0=ALU.mult, op1=ALU.add
-        )
         x_interleave(1)
         row_stats(0, 0)
         xq[1] = quantize("x1", x_words[1], HALF)
         row_stats(1, 0)
         row_stats(2, 0)
-        for g in (0, 1, 3, 2):
-            first(g, 1)
         w2_words = sbt("w2_words", [P, M, PACK], BF16)
         interleave(nc.scalar.copy, w2_words, w2_raw, 0, M)
+        w2q = quantize("w2", w2_words, M)
+        row_stats(3, 0)
+        for g in range(G):
+            first(g, 1)
+        second(0, 0)
+        second(0, 1)
+        for h in range(HALVES):
+            for g in range(1, G):
+                second(g, h)
         add_eps(0)
         add_eps(1)
+        nc.scalar.activation(out=minus_gn[:], in_=vecs[:, 0 : G * ROWS : ROWS], func=ACT.Copy, scale=-1.0)
         wo_words = sbt("wo_words", [P, O, PACK], BF16)
         interleave(nc.scalar.copy, wo_words, wo_raw, 0, O)
         add_eps(2)
+        add_eps(3)
         row_stats(0, 1)
         row_stats(1, 1)
         aggregate(0)
@@ -198,38 +204,29 @@ def tile_rows_frowcentre_kernel(tc, x, w1, w2, gn, hs, wo2, res, out):
         row_stats(2, 1)
         aggregate(1)
         shift(1)
-        row_stats(3, 0)
-        add_eps(3)
+        row_stats(3, 1)
         aggregate(2)
         shift(2)
         spread(1, 3)
-        row_stats(3, 1)
-        fold(0)
-        w2q = quantize("w2", w2_words, M)
         aggregate(3)
         spread(3, 4)
-        last = ROWS * (G - 1)
-        nc.gpsimd.tensor_scalar(
-            out=vecs[:, last + 1 : last + 2], in0=mean_var[:, G - 1, 0:1],
-            scalar1=vecs[:, last : last + 1], scalar2=-1.0, op0=ALU.mult, op1=ALU.mult,
-        )
-        nc.gpsimd.tensor_scalar(
-            out=affine[G - 1][:], in0=vecs[:, last : last + 2],
-            scalar1=rstd[:, G - 1 : G], scalar2=1.0, op0=ALU.mult, op1=ALU.mult,
-        )
-        second(0, 0)
-        second(0, 1)
-        for h in range(HALVES):
-            for g in range(1, G):
-                second(g, h)
+        fold(0)
         tanh(0, 0, N)
+        shift(3)
         fold(1)
         fold(2)
         hidden(0, 0, N)
-        for h in range(HALVES):
-            for g in range(1, G):
-                tanh(g, h * HALF, (h + 1) * HALF)
-                hidden(g, h * HALF, (h + 1) * HALF)
+        tanh(1, 0, HALF)
+        tanh(2, 0, HALF)
+        last = ROWS * (G - 1)
+        nc.vector.tensor_scalar_mul(out=affine[G - 1][:], in0=vecs[:, last : last + 2], scalar1=rstd[:, G - 1 : G])
+        hidden(1, 0, HALF)
+        hidden(2, 0, HALF)
+        tanh(3, 0, HALF)
+        hidden(3, 0, HALF)
+        for g in range(1, G):
+            tanh(g, HALF, N)
+            hidden(g, HALF, N)
         woq = quantize("wo", wo_words, O)
         h_interleave(0)
         third(0)

from contextlib import ExitStack

import concourse.mybir as mybir

G, D, M, O, N = 4, 128, 128, 128, 512
FLOPS = 2 * G * N * (2 * D * M + M * O)

F32 = mybir.dt.float32
BF16 = mybir.dt.bfloat16
U32 = mybir.dt.uint32
U8 = mybir.dt.uint8
FP8X4 = mybir.dt.float8_e4m3fn_x4
ACT = mybir.ActivationFunctionType
ALU = mybir.AluOpType

P = 128
ROWS = 32
PACK = 4
HALVES = 2
HALF = N // HALVES
MM_N = 128
EPS = 0.05
X_VECTOR = 176
H_VECTOR = (160, 160)


def tile_rows_frowcentre_kernel(tc, x, w1, w2, gn, hs, wo2, res, out):
    nc = tc.nc
    with ExitStack() as ctx:
        sb = ctx.enter_context(tc.tile_pool(name="sb", bufs=1))
        ps = ctx.enter_context(tc.psum_pool(name="ps", bufs=1))
        ctx.enter_context(tc.manual_schedule())

        def sbt(name, shape, dtype):
            return sb.tile(shape, dtype, name=name, align_bytes=64)

        def interleave(copy, dst, src, c0, c1):
            copy(
                out=dst[:, c0:c1, :].rearrange("p (c i) t -> p c t i", i=4),
                in_=src[:, :, c0:c1].rearrange("p t (c i) -> p c t i", i=4),
            )

        def quantize(name, words, width):
            codes = sbt(name + "_codes", [P, width], U32)
            scales = sbt(name + "_scales", [P, width], U8)
            nc.vector.quantize_mx(
                out=codes[:].bitcast(FP8X4),
                scales=scales[:],
                in_=words[:].rearrange("p c t -> p (c t)"),
            )
            return codes, scales

        def product(dst, col0, g, weights, moving):
            rows = slice(ROWS * g, ROWS * (g + 1))
            for c in range(0, HALF, MM_N):
                nc.tensor.matmul_mx(
                    out=dst[:, col0 + c : col0 + c + MM_N],
                    lhsT=weights[0][rows, :].bitcast(FP8X4),
                    lhsT_scale=weights[1][rows, :],
                    rhs=moving[0][rows, c : c + MM_N].bitcast(FP8X4),
                    rhs_scale=moving[1][rows, c : c + MM_N],
                    start=True,
                    stop=True,
                )

        def load_packed(name, src, c0, c1):
            raw = sbt(name, [P, PACK, c1 - c0], F32)
            nc.sync.dma_start(out=raw[:], in_=src.rearrange("g (p t) c -> (g p) t c", t=PACK)[:, :, c0:c1])
            return raw

        vec_rows = sbt("vec_rows", [P, G * ROWS], F32)
        nc.gpsimd.memset(vec_rows[:], 0.0)
        minus_half = sbt("minus_half", [P, 2], F32)
        nc.gpsimd.memset(minus_half[:], -0.5)
        w1_raw = load_packed("w1_raw", w1, 0, M)
        x_raw = [load_packed("x_raw0", x, 0, HALF)]
        for row, vec in ((0, gn), (2, hs)):
            nc.sync.dma_start(
                out=vec_rows[row:P:ROWS, :].rearrange("q (g c) -> q g c", c=ROWS),
                in_=vec.rearrange("g (q c) o -> q g (c o)", c=ROWS),
            )
        x_raw.append(load_packed("x_raw1", x, HALF, N))
        w2_raw = load_packed("w2_raw", w2, 0, M)
        wo_raw = load_packed("wo_raw", wo2, 0, O)
        res_sb = sbt("res_sb", [P, G, N], F32)
        nc.sync.dma_start(out=res_sb[:], in_=res.rearrange("g o n -> o g n"))

        bank = [[ps.tile([P, N], F32, name="bank%d%d" % (g, i)) for i in range(2)] for g in range(G)]

        vecs = sbt("vecs", [P, G * ROWS], F32)
        w1_words = sbt("w1_words", [P, M, PACK], BF16)
        interleave(nc.vector.tensor_copy, w1_words, w1_raw, 0, M)
        minus_gn = sbt("minus_gn", [P, G], F32)
        w1q = quantize("w1", w1_words, M)

        x_words = [sbt("x_words%d" % h, [P, HALF, PACK], BF16) for h in range(HALVES)]
        xq = [None] * HALVES
        stats = [sbt("stats%d" % g, [P, 16], F32) for g in range(G)]
        mean_var = sbt("mean_var", [P, G, 2], F32)
        rstd = sbt("rstd", [P, G], F32)
        affine = [sbt("affine%d" % g, [P, 2], F32) for g in range(G)]
        gate = [sbt("gate%d" % g, [P, N], F32) for g in range(G)]
        hh = [sbt("hh%d" % g, [P, N], BF16) for g in range(G)]
        hh_rows = sbt("hh_rows", [P, PACK, N], BF16)
        hh_words = [sbt("hh_words%d" % h, [P, HALF, PACK], BF16) for h in range(HALVES)]

        def x_interleave(h):
            interleave(nc.scalar.copy, x_words[h], x_raw[h], X_VECTOR, HALF)
            interleave(nc.vector.tensor_copy, x_words[h], x_raw[h], 0, X_VECTOR)

        def first(g, h):
            product(bank[g][0], h * HALF, g, w1q, xq[h])

        def second(g, h):
            product(bank[g][1], h * HALF, g, w2q, xq[h])

        def row_stats(g, h):
            nc.vector.bn_stats(out=stats[g][:, 2 + 6 * h : 8 + 6 * h], in_=bank[g][0][:, h * HALF : (h + 1) * HALF])

        def add_eps(g):
            nc.scalar.activation(out=stats[g][:, 4:5], in_=stats[g][:, 4:5], func=ACT.Copy, bias=EPS * N)

        def aggregate(g):
            nc.vector.bn_aggr(out=mean_var[:, g, :], in_=stats[g][:, 2:14])

        def shift(g):
            nc.scalar.activation(
                out=vecs[:, ROWS * g + 1 : ROWS * g + 2], in_=mean_var[:, g, 0:1], func=ACT.Copy,
                scale=minus_gn[:, g : g + 1],
            )

        def spread(g0, g1):
            nc.gpsimd.tensor_tensor(
                out=rstd[:, g0:g1], in0=mean_var[:, g0:g1, 1], in1=minus_half[:, 0 : g1 - g0], op=ALU.pow
            )

        def fold(g):
            nc.scalar.activation(
                out=affine[g][:], in_=vecs[:, ROWS * g : ROWS * g + 2], func=ACT.Copy, scale=rstd[:, g : g + 1]
            )

        def tanh(g, c0, c1):
            nc.scalar.activation(
                out=gate[g][:, c0:c1], in_=bank[g][0][:, c0:c1],
                func=ACT.Tanh, scale=affine[g][:, 0:1], bias=affine[g][:, 1:2],
            )

        def hidden(g, c0, c1):
            nc.vector.scalar_tensor_tensor(
                out=hh[g][:, c0:c1], in0=gate[g][:, c0:c1], scalar=vecs[:, ROWS * g + 2 : ROWS * g + 3],
                in1=bank[g][1][:, c0:c1], op0=ALU.mult, op1=ALU.mult,
            )
            nc.sync.dma_start(out=hh_rows[ROWS * g : ROWS * (g + 1), :, c0:c1], in_=hh[g][:, c0:c1])

        def h_interleave(h):
            rows = hh_rows[:, :, h * HALF : (h + 1) * HALF]
            interleave(nc.scalar.copy, hh_words[h], rows, H_VECTOR[h], HALF)
            interleave(nc.vector.tensor_copy, hh_words[h], rows, 0, H_VECTOR[h])

        def third(h):
            hq = quantize("h%d" % h, hh_words[h], HALF)
            for g in range(G):
                product(bank[g][h], 0, g, woq, hq)

        def finish(g, h):
            cols = slice(h * HALF, (h + 1) * HALF)
            y = sbt("y%d%d" % (g, h), [P, HALF], F32)
            nc.vector.tensor_tensor(out=y[:], in0=bank[g][h][:, 0:HALF], in1=res_sb[:, g, cols], op=ALU.add)
            nc.sync.dma_start(out=out[g, :, cols], in_=y[:])

        x_interleave(0)
        xq[0] = quantize("x0", x_words[0], HALF)
        for g in range(G):
            first(g, 0)
        nc.vector.transpose(vecs[:], vec_rows[:])
        x_interleave(1)
        row_stats(0, 0)
        xq[1] = quantize("x1", x_words[1], HALF)
        row_stats(1, 0)
        row_stats(2, 0)
        w2_words = sbt("w2_words", [P, M, PACK], BF16)
        interleave(nc.scalar.copy, w2_words, w2_raw, 0, M)
        w2q = quantize("w2", w2_words, M)
        row_stats(3, 0)
        for g in range(G):
            first(g, 1)
        second(0, 0)
        second(0, 1)
        for h in range(HALVES):
            for g in range(1, G):
                second(g, h)
        add_eps(0)
        add_eps(1)
        nc.scalar.activation(out=minus_gn[:], in_=vecs[:, 0 : G * ROWS : ROWS], func=ACT.Copy, scale=-1.0)
        wo_words = sbt("wo_words", [P, O, PACK], BF16)
        interleave(nc.scalar.copy, wo_words, wo_raw, 0, O)
        add_eps(2)
        add_eps(3)
        row_stats(0, 1)
        row_stats(1, 1)
        aggregate(0)
        shift(0)
        spread(0, 1)
        row_stats(2, 1)
        aggregate(1)
        shift(1)
        row_stats(3, 1)
        aggregate(2)
        shift(2)
        spread(1, 3)
        aggregate(3)
        spread(3, 4)
        fold(0)
        tanh(0, 0, N)
        shift(3)
        fold(1)
        fold(2)
        hidden(0, 0, N)
        tanh(1, 0, HALF)
        tanh(2, 0, HALF)
        last = ROWS * (G - 1)
        nc.vector.tensor_scalar_mul(out=affine[G - 1][:], in0=vecs[:, last : last + 2], scalar1=rstd[:, G - 1 : G])
        hidden(1, 0, HALF)
        hidden(2, 0, HALF)
        tanh(3, 0, HALF)
        hidden(3, 0, HALF)
        for g in range(1, G):
            tanh(g, HALF, N)
            hidden(g, HALF, N)
        woq = quantize("wo", wo_words, O)
        h_interleave(0)
        third(0)
        h_interleave(1)
        finish(0, 0)
        third(1)
        for g in range(1, G):
            finish(g, 0)
        for g in range(G):
            finish(g, 1)
